import numpy as np
import ml_dtypes


def mxq(x, axis, fmt="e4m3"):
    dtype, down = {"e4m3": (ml_dtypes.float8_e4m3fn, 7), "e5m2": (ml_dtypes.float8_e5m2, 14)}[fmt]
    v = np.moveaxis(np.asarray(x, np.float32).astype(ml_dtypes.bfloat16).astype(np.float64), axis, -1)
    blocks = v.reshape(v.shape[:-1] + (-1, 32))
    amax = np.abs(blocks).max(-1, keepdims=True)
    byte = np.maximum(np.where(amax > 0, np.frexp(amax)[1] - 1 + 127, 0) - down, 1)
    scale = np.exp2(byte - 127.0)
    codes = (blocks / scale).astype(np.float32).astype(dtype).astype(np.float64)
    return np.moveaxis((codes * scale).reshape(v.shape), -1, axis)


WIDE = False


def mx_kscale(k):
    if not WIDE:
        return np.ones(k)
    levels = np.array([30, -30])
    if k % 512:
        return np.exp2(np.random.permutation(np.resize(levels, k // 32))).repeat(32)
    a = np.empty((k // 512, 16))
    for p in range(k // 512):
        a[p, :8] = np.random.permutation(np.resize(levels, 8))
        for g in range(8):
            far = levels[np.abs(levels - a[p, g]) >= 10]
            a[p, g + 8] = far[np.random.randint(len(far))]
    return np.exp2(a.ravel()).repeat(32)


def f64(x):
    return np.asarray(x).astype(np.float64)


def striped(idx):
    return np.tile(np.asarray(idx).reshape(-1, 16).T, (8, 1)).astype(np.uint16)


def unstriped(offs):
    return offs[:16].T.reshape(-1).astype(np.int64)


E2M1 = np.array([0.0, 0.5, 1.0, 1.5, 2.0, 3.0, 4.0, 6.0, -0.0, -0.5, -1.0, -1.5, -2.0, -3.0, -4.0, -6.0])


def pack_weight(w, fmt):
    k, n = w.shape
    w = f64(np.asarray(w, np.float32).astype(ml_dtypes.bfloat16)).reshape(k // 32, 32, n)
    amax = np.abs(w).max(1)
    if fmt in ("e4m3", "e5m2"):
        byte = np.frexp(amax)[1] - 1 + 127 - (7 if fmt == "e4m3" else 14)
    else:
        mant, ex = np.frexp(amax / 6.0)
        byte = np.where(mant > 0.5, ex, ex - 1) + 127
    byte = np.clip(np.where(amax > 0, byte, 1), 1, 254)
    scaled = (w * np.exp2(127.0 - byte)[:, None, :]).reshape(k, n).astype(np.float32)
    by_word = np.ascontiguousarray(scaled.reshape(k // 512, 128, 4, n).transpose(0, 1, 3, 2))
    if fmt in ("e4m3", "e5m2"):
        words = by_word.astype(ml_dtypes.float8_e4m3fn if fmt == "e4m3" else ml_dtypes.float8_e5m2).view(np.uint8)
    else:
        c = by_word.astype(ml_dtypes.float4_e2m1fn).view(np.uint8) & 0xF
        words = (c[..., 0::2] | (c[..., 1::2] << 4)).reshape(k // 512, 128, 2 * n)
    return np.ascontiguousarray(words), np.ascontiguousarray(byte.astype(np.uint8).reshape(k // 512, 16, n))


def unpack_weight(words, scales, fmt):
    g, _, n = scales.shape
    words = np.ascontiguousarray(words).reshape(g, 128, n, -1)
    if fmt in ("e4m3", "e5m2"):
        vals = words.view(ml_dtypes.float8_e4m3fn if fmt == "e4m3" else ml_dtypes.float8_e5m2).astype(np.float64)
    else:
        nib = np.empty((g, 128, n, 4), np.uint8)
        nib[..., 0::2] = words & 0xF
        nib[..., 1::2] = words >> 4
        vals = E2M1[nib]
    vals = vals * np.repeat(np.exp2(scales.astype(np.float64) - 127.0), 8, axis=1)[..., None]
    return vals.transpose(0, 1, 3, 2).reshape(g * 512, n)


K, T, I, J, N, Z, S = 512, 1024, 512, 256, 256, 1024, 1024


def setup_inputs():
    n = np.random.standard_normal
    idx = np.random.permutation(T)[:I]
    idx2 = np.random.permutation(Z)[:J]
    idx3 = np.random.permutation(Z)[:J]
    idx4 = np.random.permutation(S)[:N]
    fk = mx_kscale(K)
    fi = mx_kscale(I)
    ti = np.ones(T)
    ti[idx] = fi
    xkp = pack_weight(n((K, T)) * 0.3 * fk[:, None] * ti, "e5m2")
    xqp = pack_weight(n((K, Z)) * 0.3 / fk[:, None], "e2m1")
    vsp = pack_weight(n((I, S)) / fi[:, None], "e5m2")
    return {
        "xk_words": xkp[0],
        "xk_scales": xkp[1],
        "xq_words": xqp[0],
        "xq_scales": xqp[1],
        "vs_words": vsp[0],
        "vs_scales": vsp[1],
        "offs": striped(idx),
        "offs2": striped(idx2),
        "offs3": striped(idx3),
        "offs4": striped(idx4),
    }


def reference(xk_words, xk_scales, xq_words, xq_scales, vs_words, vs_scales, offs, offs2, offs3, offs4):
    idx = unstriped(offs)
    idx2 = unstriped(offs2)
    idx3 = unstriped(offs3)
    idx4 = unstriped(offs4)
    xku = unpack_weight(xk_words, xk_scales, "e5m2")
    xqu = unpack_weight(xq_words, xq_scales, "e2m1")
    vsu = unpack_weight(vs_words, vs_scales, "e5m2")
    xkidxg = xku[:, idx]
    xqidx2g = xqu[:, idx2]
    s1 = xkidxg.T @ xqidx2g
    xqidx3g = xqu[:, idx3]
    s2 = xkidxg.T @ xqidx3g
    hid = np.abs(s1 - s2)
    vsidx4g = vsu[:, idx4]
    hidq = mxq(hid, 0, "e4m3")
    y = vsidx4g.T @ hidq
    return y

@@ -1,0 +1,148 @@
+from contextlib import ExitStack
+
+import concourse.mybir as mybir
+
+K, T, I, J, N = 512, 1024, 512, 256, 256
+FLOPS = 2 * K * I * J * 2 + 2 * I * N * J
+
+F32 = mybir.dt.float32
+BF16 = mybir.dt.bfloat16
+I32 = mybir.dt.int32
+U32 = mybir.dt.uint32
+U16 = mybir.dt.uint16
+U8 = mybir.dt.uint8
+E4M3 = mybir.dt.float8_e4m3fn_x4
+E5M2 = mybir.dt.float8_e5m2_x4
+E2M1 = mybir.dt.float4_e2m1fn_x4
+ACT = mybir.ActivationFunctionType
+ALU = mybir.AluOpType
+
+P = 128
+PACK = 4
+QUADS = 4
+HALF = 128
+
+
+def tile_list_contest_twice_direct_plain_kernel(
+    tc, xk_words, xk_scales, xq_words, xq_scales, vs_words, vs_scales, offs, offs2, offs3, offs4, out
+):
+    nc = tc.nc
+    with ExitStack() as ctx:
+        keep = ctx.enter_context(tc.tile_pool(name="keep", bufs=1))
+        psum = ctx.enter_context(tc.psum_pool(name="psum", bufs=1))
+
+        def sb(name, shape, dtype, tag=""):
+            return keep.tile(shape, dtype, name=name, tag=tag, align_bytes=64)
+
+        list_k = keep.tile([P, I // 16], U16, name="list_k")
+        list_q1 = keep.tile([P, J // 16], U16, name="list_q1")
+        list_q2 = keep.tile([P, J // 16], U16, name="list_q2")
+        list_v = keep.tile([P, N // 16], U16, name="list_v")
+        k_words, k_scales = sb("k_words", [P, T], U32, "kw"), sb("k_scales", [P, T], U8, "ks")
+        q_words, q_scales = sb("q_words", [P, T], U16), sb("q_scales", [P, T], U8, "qs")
+        v_words, v_scales = sb("v_words", [P, T], U32), sb("v_scales", [P, T], U8, "vs")
+
+        def load_scale_rows(queue, plane, rows):
+            for quad in range(QUADS):
+                queue.dma_start(
+                    out=plane[32 * quad : 32 * quad + 4, :].bitcast(I32),
+                    in_=rows[0, 4 * quad : 4 * quad + 4, :].bitcast(I32),
+                )
+
+        for plane in (k_scales, q_scales, v_scales):
+            nc.vector.memset(plane[:].bitcast(I32), 0)
+
+        nc.sync.dma_start(list_k[:], offs)
+        load_scale_rows(nc.scalar, k_scales, xk_scales)
+        nc.sync.dma_start(
+            out=k_words[:].bitcast(I32), in_=xk_words[0].rearrange("p c r -> p (c r)").bitcast(I32)
+        )
+        nc.sync.dma_start(list_q1[:], offs2)
+        nc.sync.dma_start(out=q_words[:].bitcast(I32), in_=xq_words[0].bitcast(I32))
+        load_scale_rows(nc.sync, q_scales, xq_scales)
+        nc.sync.dma_start(list_q2[:], offs3)
+        nc.sync.dma_start(
+            out=v_words[:].bitcast(I32), in_=vs_words[0].rearrange("p c r -> p (c r)").bitcast(I32)
+        )
+        nc.sync.dma_start(list_v[:], offs4)
+        load_scale_rows(nc.sync, v_scales, vs_scales)
+
+        def gather(dst, window, offsets):
+            nc.vector.tensor_copy(out=dst, in_=window[:].indirect(offsets[:]))
+
+        q1_w, q1_s = sb("q1_w", [P, J], U16), sb("q1_s", [P, J], U8)
+        k_w, k_s = sb("k_w", [P, PACK, P], U32), sb("k_s", [P, PACK, P], U8)
+
+        def scores(name, q_w, q_s):
+            banks = []
+            for h in range(J // HALF):
+                cols = slice(h * HALF, (h + 1) * HALF)
+                bank = psum.tile([P, PACK, HALF], F32, name=name + str(h))
+                for t in range(PACK):
+                    nc.tensor.matmul_mx(
+                        out=bank[:, t, :],
+                        lhsT=k_w[:, t, :].bitcast(E5M2),
+                        lhsT_scale=k_s[:, t, :],
+                        rhs=q_w[:, cols].bitcast(E2M1),
+                        rhs_scale=q_s[:, cols],
+                        start=True,
+                        stop=True,
+                    )
+                banks.append(bank)
+            return banks
+
+        gather(k_s[:].rearrange("p t m -> p m t"), k_scales, list_k)
+        gather(k_w[:].rearrange("p t m -> p m t"), k_words, list_k)
+        gather(q1_w[:], q_words, list_q1)
+        gather(q1_s[:], q_scales, list_q1)
+        s1 = scores("s1_", q1_w, q1_s)
+        s1_sb = []
+        for h in range(J // HALF):
+            kept = sb("s1_sb%d" % h, [P, HALF, PACK], F32, "s1_sb%d" % h)
+            nc.scalar.activation(out=kept[:], in_=s1[h][:].rearrange("p t j -> p j t"), func=ACT.Copy)
+            s1_sb.append(kept)
+
+        q2_w, q2_s = sb("q2_w", [P, J], U16, "ks"), sb("q2_s", [P, J], U8, "kw")
+        gather(q2_w[:], q_words, list_q2)
+        gather(q2_s[:], q_scales, list_q2)
+        s2 = scores("s2_", q2_w, q2_s)
+        v_w = sb("v_w", [P, N], U32, "qs")
+        gather(v_w[:], v_words, list_v)
+
+        hid = []
+        for h in range(J // HALF):
+            diff = sb("diff%d" % h, [P, HALF, PACK], F32)
+            nc.vector.tensor_tensor(
+                out=diff[:], in0=s2[h][:].rearrange("p t j -> p j t"), in1=s1_sb[h][:], op=ALU.subtract
+            )
+            rounded = sb("hid%d" % h, [P, HALF * PACK], BF16)
+            nc.scalar.activation(out=rounded[:], in_=diff[:].rearrange("p j t -> p (j t)"), func=ACT.Abs)
+            hid.append(rounded)
+
+        v_s = sb("v_s", [P, N], U8, "s1_sb1")
+        gather(v_s[:], v_scales, list_v)
+
+        out_rows = out.rearrange("(g p) j -> p g j", p=P)
+        for h in range(J // HALF):
+            cols = slice(h * HALF, (h + 1) * HALF)
+            h_w, h_s = sb("h_w%d" % h, [P, HALF], U32, "vs" if h == 0 else ""), sb("h_s%d" % h, [P, HALF], U8)
+            nc.vector.quantize_mx(out=h_w[:].bitcast(E4M3), scales=h_s[:], in_=hid[h][:])
+            for g in range(N // P):
+                rows = slice(g * P, (g + 1) * P)
+                bank = psum.tile([P, HALF], F32, name="y%d%d" % (h, g))
+                nc.tensor.matmul_mx(
+                    out=bank[:],
+                    lhsT=v_w[:, rows].bitcast(E5M2),
+                    lhsT_scale=v_s[:, rows],
+                    rhs=h_w[:].bitcast(E4M3),
+                    rhs_scale=h_s[:],
+                    start=True,
+                    stop=True,
+                )
+                result = sb("y_sb%d%d" % (h, g), [P, HALF], F32)
+                if g == 0 or h == 0:
+                    nc.scalar.copy(out=result[:], in_=bank[:])
+                else:
+                    nc.vector.tensor_copy(out=result[:], in_=bank[:])
+                queue = nc.scalar if (g == 0 and h == 1) else nc.sync
+                queue.dma_start(out=out_rows[:, g, cols], in_=result[:])

@@ -39,8 +39,8 @@ def tile_list_contest_twice_direct_plain_kernel(
         list_q2 = keep.tile([P, J // 16], U16, name="list_q2")
         list_v = keep.tile([P, N // 16], U16, name="list_v")
         k_words, k_scales = sb("k_words", [P, T], U32, "kw"), sb("k_scales", [P, T], U8, "ks")
-        q_words, q_scales = sb("q_words", [P, T], U16), sb("q_scales", [P, T], U8, "qs")
-        v_words, v_scales = sb("v_words", [P, T], U32), sb("v_scales", [P, T], U8, "vs")
+        q_words, q_scales = sb("q_words", [P, T], U16, "qw"), sb("q_scales", [P, T], U8)
+        v_words, v_scales = sb("v_words", [P, T], U32), sb("v_scales", [P, T], U8)
 
         def load_scale_rows(queue, plane, rows):
             for quad in range(QUADS):
@@ -52,20 +52,20 @@ def tile_list_contest_twice_direct_plain_kernel(
         for plane in (k_scales, q_scales, v_scales):
             nc.vector.memset(plane[:].bitcast(I32), 0)
 
+        nc.sync.dma_start(out=q_words[:].bitcast(I32), in_=xq_words[0].bitcast(I32))
+        nc.sync.dma_start(list_q1[:], offs2)
         nc.sync.dma_start(list_k[:], offs)
-        load_scale_rows(nc.scalar, k_scales, xk_scales)
+        load_scale_rows(nc.sync, k_scales, xk_scales)
         nc.sync.dma_start(
             out=k_words[:].bitcast(I32), in_=xk_words[0].rearrange("p c r -> p (c r)").bitcast(I32)
         )
-        nc.sync.dma_start(list_q1[:], offs2)
-        nc.sync.dma_start(out=q_words[:].bitcast(I32), in_=xq_words[0].bitcast(I32))
         load_scale_rows(nc.sync, q_scales, xq_scales)
+        load_scale_rows(nc.sync, v_scales, vs_scales)
         nc.sync.dma_start(list_q2[:], offs3)
+        nc.sync.dma_start(list_v[:], offs4)
         nc.sync.dma_start(
             out=v_words[:].bitcast(I32), in_=vs_words[0].rearrange("p c r -> p (c r)").bitcast(I32)
         )
-        nc.sync.dma_start(list_v[:], offs4)
-        load_scale_rows(nc.sync, v_scales, vs_scales)
 
         def gather(dst, window, offsets):
             nc.vector.tensor_copy(out=dst, in_=window[:].indirect(offsets[:]))
@@ -91,9 +91,9 @@ def tile_list_contest_twice_direct_plain_kernel(
                 banks.append(bank)
             return banks
 
+        gather(q1_w[:], q_words, list_q1)
         gather(k_s[:].rearrange("p t m -> p m t"), k_scales, list_k)
         gather(k_w[:].rearrange("p t m -> p m t"), k_words, list_k)
-        gather(q1_w[:], q_words, list_q1)
         gather(q1_s[:], q_scales, list_q1)
         s1 = scores("s1_", q1_w, q1_s)
         s1_sb = []
@@ -106,8 +106,8 @@ def tile_list_contest_twice_direct_plain_kernel(
         gather(q2_w[:], q_words, list_q2)
         gather(q2_s[:], q_scales, list_q2)
         s2 = scores("s2_", q2_w, q2_s)
-        v_w = sb("v_w", [P, N], U32, "qs")
-        gather(v_w[:], v_words, list_v)
+        v_s = sb("v_s", [P, N], U8, "qw")
+        gather(v_s[:], v_scales, list_v)
 
         hid = []
         for h in range(J // HALF):
@@ -119,13 +119,13 @@ def tile_list_contest_twice_direct_plain_kernel(
             nc.scalar.activation(out=rounded[:], in_=diff[:].rearrange("p j t -> p (j t)"), func=ACT.Abs)
             hid.append(rounded)
 
-        v_s = sb("v_s", [P, N], U8, "s1_sb1")
-        gather(v_s[:], v_scales, list_v)
+        v_w = sb("v_w", [P, N], U32, "s1_sb0")
+        gather(v_w[:], v_words, list_v)
 
         out_rows = out.rearrange("(g p) j -> p g j", p=P)
         for h in range(J // HALF):
             cols = slice(h * HALF, (h + 1) * HALF)
-            h_w, h_s = sb("h_w%d" % h, [P, HALF], U32, "vs" if h == 0 else ""), sb("h_s%d" % h, [P, HALF], U8)
+            h_w, h_s = sb("h_w%d" % h, [P, HALF], U32), sb("h_s%d" % h, [P, HALF], U8)
             nc.vector.quantize_mx(out=h_w[:].bitcast(E4M3), scales=h_s[:], in_=hid[h][:])
             for g in range(N // P):
                 rows = slice(g * P, (g + 1) * P)

from contextlib import ExitStack

import concourse.mybir as mybir

K, T, I, J, N = 512, 1024, 512, 256, 256
FLOPS = 2 * K * I * J * 2 + 2 * I * N * J

F32 = mybir.dt.float32
BF16 = mybir.dt.bfloat16
I32 = mybir.dt.int32
U32 = mybir.dt.uint32
U16 = mybir.dt.uint16
U8 = mybir.dt.uint8
E4M3 = mybir.dt.float8_e4m3fn_x4
E5M2 = mybir.dt.float8_e5m2_x4
E2M1 = mybir.dt.float4_e2m1fn_x4
ACT = mybir.ActivationFunctionType
ALU = mybir.AluOpType

P = 128
PACK = 4
QUADS = 4
HALF = 128


def tile_list_contest_twice_direct_plain_kernel(
    tc, xk_words, xk_scales, xq_words, xq_scales, vs_words, vs_scales, offs, offs2, offs3, offs4, out
):
    nc = tc.nc
    with ExitStack() as ctx:
        keep = ctx.enter_context(tc.tile_pool(name="keep", bufs=1))
        psum = ctx.enter_context(tc.psum_pool(name="psum", bufs=1))

        def sb(name, shape, dtype, tag=""):
            return keep.tile(shape, dtype, name=name, tag=tag, align_bytes=64)

        list_k = keep.tile([P, I // 16], U16, name="list_k")
        list_q1 = keep.tile([P, J // 16], U16, name="list_q1")
        list_q2 = keep.tile([P, J // 16], U16, name="list_q2")
        list_v = keep.tile([P, N // 16], U16, name="list_v")
        k_words, k_scales = sb("k_words", [P, T], U32, "kw"), sb("k_scales", [P, T], U8, "ks")
        q_words, q_scales = sb("q_words", [P, T], U16, "qw"), sb("q_scales", [P, T], U8)
        v_words, v_scales = sb("v_words", [P, T], U32), sb("v_scales", [P, T], U8)

        def load_scale_rows(queue, plane, rows):
            for quad in range(QUADS):
                queue.dma_start(
                    out=plane[32 * quad : 32 * quad + 4, :].bitcast(I32),
                    in_=rows[0, 4 * quad : 4 * quad + 4, :].bitcast(I32),
                )

        for plane in (k_scales, q_scales, v_scales):
            nc.vector.memset(plane[:].bitcast(I32), 0)

        nc.sync.dma_start(out=q_words[:].bitcast(I32), in_=xq_words[0].bitcast(I32))
        nc.sync.dma_start(list_q1[:], offs2)
        nc.sync.dma_start(list_k[:], offs)
        load_scale_rows(nc.sync, k_scales, xk_scales)
        nc.sync.dma_start(
            out=k_words[:].bitcast(I32), in_=xk_words[0].rearrange("p c r -> p (c r)").bitcast(I32)
        )
        load_scale_rows(nc.sync, q_scales, xq_scales)
        load_scale_rows(nc.sync, v_scales, vs_scales)
        nc.sync.dma_start(list_q2[:], offs3)
        nc.sync.dma_start(list_v[:], offs4)
        nc.sync.dma_start(
            out=v_words[:].bitcast(I32), in_=vs_words[0].rearrange("p c r -> p (c r)").bitcast(I32)
        )

        def gather(dst, window, offsets):
            nc.vector.tensor_copy(out=dst, in_=window[:].indirect(offsets[:]))

        q1_w, q1_s = sb("q1_w", [P, J], U16), sb("q1_s", [P, J], U8)
        k_w, k_s = sb("k_w", [P, PACK, P], U32), sb("k_s", [P, PACK, P], U8)

        def scores(name, q_w, q_s):
            banks = []
            for h in range(J // HALF):
                cols = slice(h * HALF, (h + 1) * HALF)
                bank = psum.tile([P, PACK, HALF], F32, name=name + str(h))
                for t in range(PACK):
                    nc.tensor.matmul_mx(
                        out=bank[:, t, :],
                        lhsT=k_w[:, t, :].bitcast(E5M2),
                        lhsT_scale=k_s[:, t, :],
                        rhs=q_w[:, cols].bitcast(E2M1),
                        rhs_scale=q_s[:, cols],
                        start=True,
                        stop=True,
                    )
                banks.append(bank)
            return banks

        gather(q1_w[:], q_words, list_q1)
        gather(k_s[:].rearrange("p t m -> p m t"), k_scales, list_k)
        gather(k_w[:].rearrange("p t m -> p m t"), k_words, list_k)
        gather(q1_s[:], q_scales, list_q1)
        s1 = scores("s1_", q1_w, q1_s)
        s1_sb = []
        for h in range(J // HALF):
            kept = sb("s1_sb%d" % h, [P, HALF, PACK], F32, "s1_sb%d" % h)
            nc.scalar.activation(out=kept[:], in_=s1[h][:].rearrange("p t j -> p j t"), func=ACT.Copy)
            s1_sb.append(kept)

        q2_w, q2_s = sb("q2_w", [P, J], U16, "ks"), sb("q2_s", [P, J], U8, "kw")
        gather(q2_w[:], q_words, list_q2)
        gather(q2_s[:], q_scales, list_q2)
        s2 = scores("s2_", q2_w, q2_s)
        v_s = sb("v_s", [P, N], U8, "qw")
        gather(v_s[:], v_scales, list_v)

        hid = []
        for h in range(J // HALF):
            diff = sb("diff%d" % h, [P, HALF, PACK], F32)
            nc.vector.tensor_tensor(
                out=diff[:], in0=s2[h][:].rearrange("p t j -> p j t"), in1=s1_sb[h][:], op=ALU.subtract
            )
            rounded = sb("hid%d" % h, [P, HALF * PACK], BF16)
            nc.scalar.activation(out=rounded[:], in_=diff[:].rearrange("p j t -> p (j t)"), func=ACT.Abs)
            hid.append(rounded)

        v_w = sb("v_w", [P, N], U32, "s1_sb0")
        gather(v_w[:], v_words, list_v)

        out_rows = out.rearrange("(g p) j -> p g j", p=P)
        for h in range(J // HALF):
            cols = slice(h * HALF, (h + 1) * HALF)
            h_w, h_s = sb("h_w%d" % h, [P, HALF], U32), sb("h_s%d" % h, [P, HALF], U8)
            nc.vector.quantize_mx(out=h_w[:].bitcast(E4M3), scales=h_s[:], in_=hid[h][:])
            for g in range(N // P):
                rows = slice(g * P, (g + 1) * P)
                bank = psum.tile([P, HALF], F32, name="y%d%d" % (h, g))
                nc.tensor.matmul_mx(
                    out=bank[:],
                    lhsT=v_w[:, rows].bitcast(E5M2),
                    lhsT_scale=v_s[:, rows],
                    rhs=h_w[:].bitcast(E4M3),
                    rhs_scale=h_s[:],
                    start=True,
                    stop=True,
                )
                result = sb("y_sb%d%d" % (h, g), [P, HALF], F32)
                if g == 0 or h == 0:
                    nc.scalar.copy(out=result[:], in_=bank[:])
                else:
                    nc.vector.tensor_copy(out=result[:], in_=bank[:])
                queue = nc.scalar if (g == 0 and h == 1) else nc.sync
                queue.dma_start(out=out_rows[:, g, cols], in_=result[:])
